import numpy as np
import ml_dtypes


def mxq(x, axis, fmt="e4m3"):
    dtype, down = {"e4m3": (ml_dtypes.float8_e4m3fn, 7), "e5m2": (ml_dtypes.float8_e5m2, 14)}[fmt]
    v = np.moveaxis(np.asarray(x, np.float32).astype(ml_dtypes.bfloat16).astype(np.float64), axis, -1)
    blocks = v.reshape(v.shape[:-1] + (-1, 32))
    amax = np.abs(blocks).max(-1, keepdims=True)
    byte = np.maximum(np.where(amax > 0, np.frexp(amax)[1] - 1 + 127, 0) - down, 1)
    scale = np.exp2(byte - 127.0)
    codes = (blocks / scale).astype(np.float32).astype(dtype).astype(np.float64)
    return np.moveaxis((codes * scale).reshape(v.shape), -1, axis)


WIDE = False


def mx_kscale(k):
    if not WIDE:
        return np.ones(k)
    levels = np.array([30, -30])
    if k % 512:
        return np.exp2(np.random.permutation(np.resize(levels, k // 32))).repeat(32)
    a = np.empty((k // 512, 16))
    for p in range(k // 512):
        a[p, :8] = np.random.permutation(np.resize(levels, 8))
        for g in range(8):
            far = levels[np.abs(levels - a[p, g]) >= 10]
            a[p, g + 8] = far[np.random.randint(len(far))]
    return np.exp2(a.ravel()).repeat(32)


BF16 = ml_dtypes.bfloat16


def bf(x):
    return np.asarray(x, np.float32).astype(BF16)


def f64(x):
    return np.asarray(x).astype(np.float64)


E2M1 = np.array([0.0, 0.5, 1.0, 1.5, 2.0, 3.0, 4.0, 6.0, -0.0, -0.5, -1.0, -1.5, -2.0, -3.0, -4.0, -6.0])


def pack_weight(w, fmt):
    k, n = w.shape
    w = f64(bf(w)).reshape(k // 32, 32, n)
    amax = np.abs(w).max(1)
    if fmt in ("e4m3", "e5m2"):
        byte = np.frexp(amax)[1] - 1 + 127 - (7 if fmt == "e4m3" else 14)
    else:
        mant, ex = np.frexp(amax / 6.0)
        byte = np.where(mant > 0.5, ex, ex - 1) + 127
    byte = np.clip(np.where(amax > 0, byte, 1), 1, 254)
    scaled = (w * np.exp2(127.0 - byte)[:, None, :]).reshape(k, n).astype(np.float32)
    by_word = np.ascontiguousarray(scaled.reshape(k // 512, 128, 4, n).transpose(0, 1, 3, 2))
    if fmt in ("e4m3", "e5m2"):
        words = by_word.astype(ml_dtypes.float8_e4m3fn if fmt == "e4m3" else ml_dtypes.float8_e5m2).view(np.uint8)
    else:
        c = by_word.astype(ml_dtypes.float4_e2m1fn).view(np.uint8) & 0xF
        words = c[..., 0::2] | (c[..., 1::2] << 4)
    return np.ascontiguousarray(words), np.ascontiguousarray(byte.astype(np.uint8).reshape(k // 512, 16, n))


def unpack_weight(words, scales, fmt):
    g, p, n, _ = words.shape
    if fmt in ("e4m3", "e5m2"):
        vals = np.ascontiguousarray(words).view(ml_dtypes.float8_e4m3fn if fmt == "e4m3" else ml_dtypes.float8_e5m2).astype(np.float64)
    else:
        nib = np.empty((g, p, n, 4), np.uint8)
        nib[..., 0::2] = words & 0xF
        nib[..., 1::2] = words >> 4
        vals = E2M1[nib]
    vals = vals * np.repeat(np.exp2(scales.astype(np.float64) - 127.0), 8, axis=1)[..., None]
    return vals.transpose(0, 1, 3, 2).reshape(g * 512, n)


D, Q, P, F = 2048, 1024, 1024, 512


def setup_inputs():
    s, t, u = mx_kscale(Q), mx_kscale(P), mx_kscale(D)
    G = 0.7 * np.random.standard_t(4, (Q, D)) * s[:, None]
    G_words, G_scales = pack_weight(G, "e5m2")
    jac = np.random.standard_normal((Q, P)) / np.sqrt(Q)
    slope = 1.0 / (1.0 + np.exp(-np.random.standard_normal((D, P))))
    load = np.random.standard_normal((P, F)) / np.sqrt(P)
    fac = np.random.standard_normal((D, F)) / np.sqrt(D)
    rate_day = 1.0 + 0.1 * np.random.standard_normal(D)
    rate_node = 1.0 + 0.1 * np.random.standard_normal(P)
    return {"g_words": G_words, "g_scales": G_scales,
            "jac": bf(jac / s[:, None] * t),
            "slope": bf(slope * u[:, None]),
            "load": bf(load / t[:, None]),
            "fac": bf(fac / u[:, None]),
            "rate_day": bf(rate_day / u),
            "rate_node": bf(rate_node / t)}


def reference(g_words, g_scales, jac, slope, load, fac, rate_day, rate_node):
    res = unpack_weight(g_words, g_scales, "e5m2")
    dnode = res.T @ mxq(f64(jac), 0, "e4m3")
    dz = dnode * f64(slope)
    dfac = mxq(dz, 1, "e5m2") @ mxq(f64(load), 0, "e4m3")
    dload = mxq(dz, 0, "e5m2").T @ mxq(f64(fac), 0, "e4m3")
    return dfac * f64(rate_day)[:, None], dload * f64(rate_node)[:, None]

@@ -1,0 +1,271 @@
+from contextlib import ExitStack
+
+import concourse.mybir as mybir
+from concourse.masks import make_identity
+
+D, Q, P, F = 2048, 1024, 1024, 512
+FLOPS = 2 * D * Q * P + 2 * 2 * D * P * F
+
+F32 = mybir.dt.float32
+BF16 = mybir.dt.bfloat16
+I32 = mybir.dt.int32
+U32 = mybir.dt.uint32
+U8 = mybir.dt.uint8
+E4 = mybir.dt.float8_e4m3fn_x4
+E5 = mybir.dt.float8_e5m2_x4
+MULT = mybir.AluOpType.mult
+COPY = mybir.ActivationFunctionType.Copy
+
+
+def tile_volatility_calibration_gradients_e3_kernel(
+    tc, g_words, g_scales, jac, slope, load, fac, rate_day, rate_node, out_0, out_1
+):
+    nc = tc.nc
+    with ExitStack() as ctx:
+        keep = ctx.enter_context(tc.tile_pool(name="keep", bufs=1))
+        work = ctx.enter_context(tc.tile_pool(name="work", bufs=2))
+        psum = ctx.enter_context(tc.psum_pool(name="psum", bufs=2))
+
+        def kt(name, shape, dt):
+            return keep.tile(shape, dt, name=name, align_bytes=64)
+
+        ident = kt("ident", [128, 128], F32)
+        g_raw = [kt(f"graw{h}", [128, 2, 512], I32) for h in range(4)]
+        g_perm = [kt(f"gperm{h}", [128, 2, 4, 128], I32) for h in range(4)]
+        gs_raw = kt("gsraw", [128, 2, 2048], U8)
+        gs_perm = [kt(f"gsperm{h}", [128, 2, 4, 128], U8) for h in range(4)]
+        slope_sb = [kt(f"slope{h}", [128, 4, 1024], BF16) for h in range(4)]
+        jac_raw = [[kt(f"jacraw{n}{g}", [128, 4, 512], BF16) for g in range(2)] for n in range(2)]
+        load_raw = [kt(f"loadraw{n}", [128, 4, 512], BF16) for n in range(2)]
+        fac_raw = [kt(f"facraw{h}", [128, 4, 512], BF16) for h in range(4)]
+        jac_q = [[(kt(f"jacq{n}{g}", [128, 512], U32), kt(f"jacs{n}{g}", [128, 512], U8)) for g in range(2)] for n in range(2)]
+        load_q = [(kt(f"loadq{n}", [128, 512], U32), kt(f"loads{n}", [128, 512], U8)) for n in range(2)]
+        fac_q = [(kt(f"facq{h}", [128, 512], U32), kt(f"facs{h}", [128, 512], U8)) for h in range(4)]
+        zb_q = [[(kt(f"zbq{h}{n}", [128, 512], U32), kt(f"zbs{h}{n}", [128, 512], U8)) for n in range(2)] for h in range(4)]
+        za_q = {}
+        rate_bf = kt("ratebf", [128, 24], BF16)
+        rate = kt("rate", [128, 24], F32)
+
+        def vcopy(o, i):
+            nc.vector.tensor_copy(out=o, in_=i)
+
+        def scopy(o, i):
+            nc.scalar.copy(out=o, in_=i)
+
+        nc.vector.memset(gs_raw[:].rearrange("p g n -> p (g n)").bitcast(I32), 0)
+        make_identity(nc, ident[:])
+
+        def ld(o, i):
+            nc.sync.dma_start(out=o, in_=i)
+
+        def ld_jac(n, g):
+            ld(jac_raw[n][g][:], jac[512 * g : 512 * g + 512, 512 * n : 512 * n + 512].rearrange("(p j) w -> p j w", j=4))
+
+        def ld_scales():
+            rows = g_scales.rearrange("g (Q r) n -> r Q g n", r=4)
+            for r in range(4):
+                ld(gs_raw[r:128:32, :, :].bitcast(I32), rows[r].bitcast(I32))
+
+        def ld_g(h):
+            ld(g_raw[h][:], g_words.rearrange("g p n t -> p g (n t)")[:, :, 2048 * h : 2048 * h + 2048].bitcast(I32))
+
+        def ld_slope(h, c0, c1):
+            ld(slope_sb[h][:, :, c0:c1], slope[512 * h : 512 * h + 512, c0:c1].rearrange("(p t) w -> p t w", t=4))
+
+        def ld_load(n):
+            ld(load_raw[n][:], load[512 * n : 512 * n + 512, :].rearrange("(p j) w -> p j w", j=4))
+
+        def ld_fac(h):
+            ld(fac_raw[h][:], fac[512 * h : 512 * h + 512, :].rearrange("(p j) w -> p j w", j=4))
+
+        ld_jac(0, 0)
+        ld_jac(0, 1)
+        ld_g(0)
+        ld_scales()
+        ld_slope(0, 0, 512)
+        ld_jac(1, 0)
+        ld_jac(1, 1)
+        ld_slope(0, 512, 1024)
+        ld_load(0)
+        ld_load(1)
+        ld(rate_bf[:, 0:16].rearrange("p (h t) -> p h t", t=4), rate_day.rearrange("(h p t) -> p h t", h=4, t=4))
+        ld(rate_bf[:, 16:24].rearrange("p (n c) -> p n c", c=4), rate_node.rearrange("(n m c) -> m n c", n=2, c=4))
+        ld_g(1)
+        ld_slope(1, 0, 1024)
+        ld_fac(0)
+        ld_g(2)
+        ld_slope(2, 0, 1024)
+        ld_fac(1)
+        ld_g(3)
+        ld_slope(3, 0, 1024)
+        ld_fac(2)
+        ld_fac(3)
+
+        def interleave(raw, vcols):
+            grouped = work.tile([128, 512, 4], BF16, name="grouped", align_bytes=64)
+            src = raw[:].rearrange("p j (c i) -> p c j i", i=4)
+            dst = grouped[:].rearrange("p (c i) j -> p c j i", i=4)
+            for eng, c0, c1 in ((vcopy, 0, vcols // 4), (scopy, vcols // 4, (vcols // 4 + 128) // 2), (scopy, (vcols // 4 + 128) // 2, 128)):
+                if c1 > c0:
+                    eng(dst[:, c0:c1], src[:, c0:c1])
+            return grouped
+
+        def quant(grouped, q, fmt):
+            nc.vector.quantize_mx(out=q[0][:].bitcast(fmt), scales=q[1][:], in_=grouped[:].rearrange("p c j -> p (c j)"))
+
+        def perm_g(h):
+            vcopy(g_perm[h][:], g_raw[h][:].rearrange("p g (m t) -> p g t m", t=4))
+            vcopy(gs_perm[h][:], gs_raw[:, :, 512 * h : 512 * h + 512].rearrange("p g (m t) -> p g t m", t=4))
+
+        zn = {}
+        zbg = {}
+        zag = {}
+        s1 = {}
+
+        def stage1(h, n):
+            for t in range(4):
+                acc = psum.tile([128, 512], F32, name="s1", bufs=4)
+                for g in range(2):
+                    nc.tensor.matmul_mx(
+                        out=acc[:],
+                        lhsT=g_perm[h][:, g, t, :].bitcast(E5), lhsT_scale=gs_perm[h][:, g, t, :],
+                        rhs=jac_q[n][g][0][:].bitcast(E4), rhs_scale=jac_q[n][g][1][:],
+                        start=(g == 0), stop=(g == 1),
+                    )
+                s1[h, n, t] = acc
+
+        def mult(h, n):
+            z = work.tile([128, 4, 2, 128, 2], BF16, name="zn", align_bytes=64)
+            for t in range(4):
+                nc.vector.tensor_tensor(
+                    out=z[:, t],
+                    in0=s1[h, n, t][:].rearrange("p (m u e) -> p u m e", u=2, e=2),
+                    in1=slope_sb[h][:, t, 512 * n : 512 * n + 512].rearrange("p (m u e) -> p u m e", u=2, e=2),
+                    op=MULT,
+                )
+            zn[h, n] = z
+
+        def zb_half(h, n, u, eng):
+            if u == 0:
+                zbg[h, n] = work.tile([128, 2, 2, 128, 4], BF16, name="zbg", align_bytes=64)
+            eng(zbg[h, n][:, u], zn[h, n][:, :, u].rearrange("p t m e -> p e m t"))
+
+        def zb_quant(h, n):
+            q = zb_q[h][n]
+            nc.vector.quantize_mx(out=q[0][:].bitcast(E5), scales=q[1][:], in_=zbg[h, n][:].rearrange("p u e m t -> p (u e m t)"))
+
+        def turn(h, n, engs):
+            za = work.tile([128, 512, 4], BF16, name="zag", align_bytes=64)
+            words = za[:].rearrange("p c t -> p (c t)").bitcast(F32).rearrange("p (v t m u) -> p v t m u", v=2, t=2, u=2)
+            z = zn[h, n]
+            for v in range(2):
+                tp = psum.tile([128, 2, 2, 128], F32, name="tp", bufs=2)
+                for t in range(2):
+                    for u in range(2):
+                        nc.tensor.transpose(tp[:, t, u, :], z[:, 2 * v + t, u].rearrange("p m e -> p (m e)").bitcast(F32), ident[:])
+                engs[v](words[:, v], tp[:].rearrange("p t u m -> p t m u"))
+            zag[h, n] = za
+
+        def za_quant(h, n):
+            q = (work.tile([128, 512], U32, name="zaq", bufs=4, align_bytes=64), work.tile([128, 512], U8, name="zas", bufs=4, align_bytes=64))
+            quant(zag[h, n], q, E5)
+            za_q[h, n] = q
+
+        ofac = {}
+
+        def evac(eng, o, acc, col):
+            if eng == "s":
+                nc.scalar.activation(out=o, in_=acc, func=COPY, scale=rate[:, col : col + 1])
+            else:
+                nc.vector.tensor_scalar(out=o, in0=acc, scalar1=rate[:, col : col + 1], scalar2=None, op0=MULT)
+
+        def dfac(h, engs, split):
+            o = work.tile([128, 4, 512], F32, name="ofac", align_bytes=64)
+            rows = out_0[512 * h : 512 * h + 512, :].rearrange("(p t) f -> p t f", t=4)
+            for t in range(4):
+                acc = psum.tile([128, 512], F32, name="o", bufs=2)
+                for n in range(2):
+                    q = za_q[h, n]
+                    nc.tensor.matmul_mx(
+                        out=acc[:],
+                        lhsT=q[0][:, 128 * t : 128 * t + 128].bitcast(E5), lhsT_scale=q[1][:, 128 * t : 128 * t + 128],
+                        rhs=load_q[n][0][:].bitcast(E4), rhs_scale=load_q[n][1][:],
+                        start=(n == 0), stop=(n == 1),
+                    )
+                evac(engs[t], o[:, t, :], acc[:], 4 * h + t)
+                if split:
+                    nc.sync.dma_start(out=rows[:, t, :], in_=o[:, t, :])
+            if not split:
+                nc.sync.dma_start(out=rows, in_=o[:])
+
+        def dload_pass(acc, n, c, h):
+            q = zb_q[h][n]
+            nc.tensor.matmul_mx(
+                out=acc[:],
+                lhsT=q[0][:, 128 * c : 128 * c + 128].bitcast(E5), lhsT_scale=q[1][:, 128 * c : 128 * c + 128],
+                rhs=fac_q[h][0][:].bitcast(E4), rhs_scale=fac_q[h][1][:],
+                start=(h == 0), stop=(h == 3),
+            )
+
+        def dload_out(acc, n, c, eng):
+            o = work.tile([128, 512], F32, name="oload", bufs=6, align_bytes=64)
+            evac(eng, o[:], acc[:], 16 + 4 * n + c)
+            nc.sync.dma_start(out=out_1[512 * n : 512 * n + 512, :].rearrange("(m c) f -> m c f", c=4)[:, c, :], in_=o[:])
+
+        quant(interleave(jac_raw[0][0], 352), jac_q[0][0], E4)
+        perm_g(0)
+        quant(interleave(jac_raw[0][1], 352), jac_q[0][1], E4)
+        stage1(0, 0)
+        j10 = interleave(jac_raw[1][0], 0)
+        mult(0, 0)
+        j11 = interleave(jac_raw[1][1], 256)
+        quant(j10, jac_q[1][0], E4)
+        quant(j11, jac_q[1][1], E4)
+        zb_half(0, 0, 0, vcopy)
+        zb_half(0, 0, 1, scopy)
+
+        vcopy(rate[:], rate_bf[:])
+        steps = [(h, n) for h in range(4) for n in range(2)]
+        for i in range(1, 8):
+            h, n = steps[i]
+            ph, pn = steps[i - 1]
+            stage1(h, n)
+            turn(ph, pn, (scopy, scopy))
+            if n == 1 and h > 0:
+                dfac(h - 1, "ssss", False)
+            if i == 1:
+                l0 = interleave(load_raw[0], 0)
+            if n == 1 and h < 3:
+                perm_g(h + 1)
+            mult(h, n)
+            zb_half(h, n, 0, vcopy)
+            zb_half(h, n, 1, scopy)
+            za_quant(ph, pn)
+            zb_quant(ph, pn)
+            if i == 1:
+                quant(l0, load_q[0], E4)
+                l1 = interleave(load_raw[1], 0)
+                quant(l1, load_q[1], E4)
+            if i in (3, 4, 5, 6):
+                f = interleave(fac_raw[i - 3], 0)
+                quant(f, fac_q[i - 3], E4)
+        turn(3, 1, (scopy, scopy))
+        for c in range(4):
+            acc = psum.tile([128, 512], F32, name="o", bufs=2)
+            for hh in range(4):
+                dload_pass(acc, 0, c, hh)
+            if c == 0:
+                za_quant(3, 1)
+            if c == 1:
+                zb_quant(3, 1)
+            dload_out(acc, 0, c, "sv"[c % 2])
+        accs = []
+        for c in range(4):
+            acc = psum.tile([128, 512], F32, name="s1", bufs=4)
+            for hh in range(3):
+                dload_pass(acc, 1, c, hh)
+            accs.append(acc)
+        dfac(3, "svsv", True)
+        for c in range(4):
+            dload_pass(accs[c], 1, c, 3)
+            dload_out(accs[c], 1, c, "sv"[c % 2])

@@ -11,10 +11,191 @@ BF16 = mybir.dt.bfloat16
 I32 = mybir.dt.int32
 U32 = mybir.dt.uint32
 U8 = mybir.dt.uint8
-E4 = mybir.dt.float8_e4m3fn_x4
-E5 = mybir.dt.float8_e5m2_x4
+E4M3 = mybir.dt.float8_e4m3fn_x4
+E5M2 = mybir.dt.float8_e5m2_x4
 MULT = mybir.AluOpType.mult
+ADD = mybir.AluOpType.add
 COPY = mybir.ActivationFunctionType.Copy
+
+STEPS = [(h, n) for h in range(4) for n in range(2)]
+OPERANDS = [("jac", n, g) for n in range(2) for g in range(2)] + [("load", n) for n in range(2)] + [("fac", h) for h in range(4)]
+
+GROUPED, PRODUCTS, BY_DAYS, BY_NODES, RAW, SLOPES = 3, 4, 3, 2, 3, 2
+SUM_BANKS, TURN_BANKS, OUT_BLOCKS, OUT_TILES = 6, 2, 2, 7
+
+LOADS = [
+    ("jac", 0), ("scales in",), ("jac", 1), ("g", 0, 0), ("g", 0, 1), ("half slope", 0, 1),
+    ("half slope", 0, 0), ("load", 0), ("load", 1), ("g", 1, 1), ("g", 1, 0), ("slope", 1), ("fac", 0),
+    ("rates in",), ("slope", 2), ("fac", 1), ("g", 2, 0), ("g", 2, 1), ("g", 3, 0), ("g", 3, 1), ("slope", 3),
+    ("fac", 2), ("fac", 3),
+]
+
+WINDOW = 0
+ORDER = {
+    "T": ["fac sum", "turn", "load sum", "sum"],
+    "V": ["quantise days", "interleave fac", "codes", "quantise jac", "quantise nodes", "quantise load",
+          "interleave jac", "multiply", "quantise fac", "rates", "scales", "days", "fac out", "load out"],
+    "S": ["fac out", "load out", "turned", "interleave load", "interleave jac", "days", "interleave fac"],
+    "G": ["interleave fac"],
+}
+
+JAC_V = [256, 256, 256, 64]
+FAC_V, FAC_G = [(3, 1)], [(2, 0), (2, 1), (3, 0), (1, 0), (0, 1)]
+DAYS_V = [1, 0, 0, 1, 0, 2, 0, 2]
+FAC_OUT_V, LOAD_OUT_V = [(1, 1), (2, 3), (2, 2)], [(1, 3), (1, 2), (1, 0), (1, 1)]
+OPEN_SUMS = 4
+
+LENGTH = {"move": 512, "multiply": 512, "quantise": 528, "interleave V": 592, "interleave S": 1072, "interleave G": 1312,
+          "codes": 260, "scales": 504, "rates": 48, "pass": 256, "turn": 584, "switch": 112, "store": 544}
+LOAD_LENGTH = {"jac": 2010, "half slope": 1224, "slope": 2010, "load": 1036, "fac": 1036, "g": 552, "scales in": 280, "rates in": 224}
+LOAD_START, LOAD_END = 660, 1112
+LAG = {"TT": 0, "TV": 336, "TS": 336, "VT": 280, "ST": 280, "VV": 200, "VS": 136, "SV": 68, "SS": 168, "GV": 168, "VG": 168}
+
+
+def list_units():
+    units = {}
+
+    def add(name, engine, length, needs, opens=None, frees=None):
+        units[name] = (engine, length, needs, opens, frees)
+
+    for i, key in enumerate(OPERANDS):
+        free = [("quantise " + OPERANDS[i - GROUPED][0],) + OPERANDS[i - GROUPED][1:]] if i >= GROUPED else []
+        parts = []
+        for half in range(2):
+            engine, columns = share_of(key, half)
+            if columns:
+                parts.append(("interleave " + key[0],) + key[1:] + (half,))
+                add(parts[-1], engine, LENGTH["interleave " + engine] * columns // 256, [key] + free)
+        add(("quantise " + key[0],) + key[1:], "V", LENGTH["quantise"], parts)
+    add(("rates",), "V", LENGTH["rates"], [("rates in",)])
+    for h in range(4):
+        for g in range(2):
+            add(("codes", h, g), "V", LENGTH["codes"], [("g", h, g)])
+        add(("scales", h), "V", LENGTH["scales"], [("scales in",)])
+    for k, (h, n) in enumerate(STEPS):
+        products = [("multiply", k, t) for t in range(4)]
+        for t in range(4):
+            add(("sum", k, t, 0), "T", LENGTH["pass"], [("codes", h, 0), ("scales", h), ("quantise jac", n, 0)], opens=("sums", 1))
+            add(("sum", k, t, 1), "T", LENGTH["pass"], [("sum", k, t, 0), ("codes", h, 1), ("quantise jac", n, 1)])
+            free = [("turn", k - PRODUCTS), ("days", k - PRODUCTS, 0), ("days", k - PRODUCTS, 1)] if k >= PRODUCTS else []
+            add(products[t], "V", LENGTH["multiply"], [("sum", k, t, 1), ("slope", h, n)] + free, frees="sums")
+        add(("turn", k), "T", LENGTH["turn"], products, opens=("turns", 2))
+        for v in range(2):
+            free = [("quantise nodes", k - BY_NODES)] if k >= BY_NODES else []
+            add(("turned", k, v), "S", LENGTH["move"], [("turn", k)] + free, frees="turns")
+        for u in range(2):
+            engine = "V" if u < DAYS_V[k] else "S"
+            free = [("quantise days", k - BY_DAYS)] if k >= BY_DAYS else []
+            add(("days", k, u), engine, LENGTH["interleave " + engine], products + free)
+        add(("quantise nodes", k), "V", LENGTH["quantise"], [("turned", k, 0), ("turned", k, 1)])
+        add(("quantise days", k), "V", LENGTH["quantise"], [("days", k, 0), ("days", k, 1)])
+    for h in range(4):
+        for t in range(4):
+            needs = [("quantise nodes", 2 * h + n) for n in range(2)] + [("quantise load", n) for n in range(2)]
+            add(("fac sum", h, t), "T", 2 * LENGTH["pass"], needs, opens=("sums", 1))
+            add(("fac out", h, t), "V" if (h, t) in FAC_OUT_V else "S", LENGTH["move"], [("fac sum", h, t), ("rates",)], frees="sums")
+    for n in range(2):
+        for c in range(4):
+            for h in range(4):
+                needs = [("quantise days", 2 * h + n), ("quantise fac", h)] + ([("load sum", n, c, h - 1)] if h else [])
+                add(("load sum", n, c, h), "T", LENGTH["pass"], needs, opens=None if h else ("sums", 1))
+            add(("load out", n, c), "V" if (n, c) in LOAD_OUT_V else "S", LENGTH["move"], [("load sum", n, c, 3), ("rates",)], frees="sums")
+    return units
+
+
+def share_of(key, half):
+    if key[0] == "jac":
+        columns = JAC_V[2 * key[1] + key[2]]
+        return ("S", 512 - columns) if half else ("V", columns)
+    if key[0] == "fac" and (key[1], half) in FAC_V:
+        return "V", 256
+    if key[0] == "fac" and (key[1], half) in FAC_G:
+        return "G", 256
+    return "S", 256
+
+
+def parts_of(item):
+    if item[0] == "jac":
+        return [("jac", n, item[1]) for n in range(2)]
+    if item[0] == "slope":
+        return [("slope", item[1], n) for n in range(2)]
+    if item[0] == "half slope":
+        return [("slope",) + item[1:]]
+    return [item]
+
+
+def shares_port(name):
+    return name[0] not in ("multiply", "fac out", "load out")
+
+
+def plan():
+    units = list_units()
+    arrive, clock = {}, LOAD_START
+    for item in LOADS:
+        clock += LOAD_LENGTH[item[0]]
+        for part in parts_of(item):
+            arrive[part] = clock + LOAD_END
+
+    users, missing, ready = {}, {}, {}
+    done, order = {}, []
+    free_at = {"T": 0, "V": 0, "S": 0, "G": 0}
+    banks = {"sums": [0] * SUM_BANKS, "turns": [0] * TURN_BANKS}
+    port_free, stored, turning, open_sums = 0, clock, False, 0
+
+    def lag(need, engine):
+        return arrive[need] if need in arrive else done[need] + LAG[units[need][0] + engine]
+
+    def make_ready(name):
+        ready[name] = max([lag(need, units[name][0]) for need in units[name][2]])
+
+    for name in units:
+        inside = [need for need in units[name][2] if need not in arrive]
+        missing[name] = len(inside)
+        for need in inside:
+            users.setdefault(need, []).append(name)
+        if not inside:
+            make_ready(name)
+
+    while ready:
+        choices = []
+        for name in ready:
+            engine, length, needs, opens, frees = units[name]
+            start = max(free_at[engine], ready[name])
+            if opens:
+                if len(banks[opens[0]]) < opens[1]:
+                    continue
+                if name[0] == "load sum" and open_sums >= OPEN_SUMS and ("multiply", 7, 3) not in done:
+                    continue
+                start = max(start, sorted(banks[opens[0]])[opens[1] - 1])
+            if engine == "G":
+                start = max(start, port_free)
+            if engine == "V" and shares_port(name):
+                start = max(start, free_at["G"])
+            choices.append((ORDER[engine].index(name[0]), name[1:], start, name))
+        soonest = min([choice[2] for choice in choices])
+        start, name = min([choice for choice in choices if choice[2] <= soonest + WINDOW])[2:]
+        engine, length, needs, opens, frees = units[name]
+        end = start + length
+        if engine == "T" and (name[0] == "turn") != turning:
+            end += LENGTH["switch"]
+            turning = not turning
+        if engine == "V" and shares_port(name):
+            port_free = end
+        free_at[engine] = done[name] = end
+        if opens:
+            banks[opens[0]] = sorted(banks[opens[0]])[opens[1] :]
+        if frees:
+            banks[frees].append(end + LAG["TV"] // 5)
+        open_sums += (name[0] == "load sum" and name[3] == 0) - (name[0] == "load out")
+        if name[0] in ("fac out", "load out"):
+            stored = max(stored, end + LOAD_START) + LENGTH["store"]
+        ready.pop(name)
+        order.append((start, len(order), name))
+        for user in users.get(name, []):
+            missing[user] -= 1
+            if missing[user] == 0:
+                make_ready(user)
+    return [name for start, i, name in sorted(order)], stored
 
 
 def tile_volatility_calibration_gradients_e3_kernel(
@@ -25,247 +206,205 @@ def tile_volatility_calibration_gradients_e3_kernel(
         keep = ctx.enter_context(tc.tile_pool(name="keep", bufs=1))
         work = ctx.enter_context(tc.tile_pool(name="work", bufs=2))
         psum = ctx.enter_context(tc.psum_pool(name="psum", bufs=2))
+        ctx.enter_context(tc.manual_schedule())
 
-        def kt(name, shape, dt):
-            return keep.tile(shape, dt, name=name, align_bytes=64)
+        def kept(name, shape, dtype):
+            return keep.tile(shape, dtype, name=name, align_bytes=64)
 
-        ident = kt("ident", [128, 128], F32)
-        g_raw = [kt(f"graw{h}", [128, 2, 512], I32) for h in range(4)]
-        g_perm = [kt(f"gperm{h}", [128, 2, 4, 128], I32) for h in range(4)]
-        gs_raw = kt("gsraw", [128, 2, 2048], U8)
-        gs_perm = [kt(f"gsperm{h}", [128, 2, 4, 128], U8) for h in range(4)]
-        slope_sb = [kt(f"slope{h}", [128, 4, 1024], BF16) for h in range(4)]
-        jac_raw = [[kt(f"jacraw{n}{g}", [128, 4, 512], BF16) for g in range(2)] for n in range(2)]
-        load_raw = [kt(f"loadraw{n}", [128, 4, 512], BF16) for n in range(2)]
-        fac_raw = [kt(f"facraw{h}", [128, 4, 512], BF16) for h in range(4)]
-        jac_q = [[(kt(f"jacq{n}{g}", [128, 512], U32), kt(f"jacs{n}{g}", [128, 512], U8)) for g in range(2)] for n in range(2)]
-        load_q = [(kt(f"loadq{n}", [128, 512], U32), kt(f"loads{n}", [128, 512], U8)) for n in range(2)]
-        fac_q = [(kt(f"facq{h}", [128, 512], U32), kt(f"facs{h}", [128, 512], U8)) for h in range(4)]
-        zb_q = [[(kt(f"zbq{h}{n}", [128, 512], U32), kt(f"zbs{h}{n}", [128, 512], U8)) for n in range(2)] for h in range(4)]
-        za_q = {}
-        rate_bf = kt("ratebf", [128, 24], BF16)
-        rate = kt("rate", [128, 24], F32)
+        def working(name, shape, dtype, bufs):
+            return work.tile(shape, dtype, name=name, bufs=bufs, align_bytes=64)
 
-        def vcopy(o, i):
-            nc.vector.tensor_copy(out=o, in_=i)
+        def quantised(name):
+            return kept(name + "_codes", [128, 512], U32), kept(name + "_scales", [128, 512], U8)
 
-        def scopy(o, i):
-            nc.scalar.copy(out=o, in_=i)
+        identity = kept("identity", [128, 128], F32)
+        g_raw = {(h, g): kept(f"g_raw{h}{g}", [128, 512], I32) for h in range(4) for g in range(2)}
+        g_codes = {(h, g): kept(f"g_codes{h}{g}", [128, 4, 128], I32) for h in range(4) for g in range(2)}
+        g_scales_raw = kept("g_scales_raw", [128, 2, 2048], U8)
+        g_scale_rows = [kept(f"g_scale_rows{h}", [128, 2, 4, 128], U8) for h in range(4)]
+        inputs_q = {key: quantised("_".join([str(part) for part in key])) for key in OPERANDS}
+        by_days_q = [quantised(f"by_days{k}") for k in range(8)]
+        by_nodes_q = [quantised(f"by_nodes{k}") for k in range(8)]
+        rates_in = kept("rates_in", [128, 24], BF16)
+        rates = kept("rates", [128, 24], F32)
+        slopes, raw, grouped, sums, products, turned, by_nodes, by_days, out_block, block_filled = {}, {}, {}, {}, {}, {}, {}, {}, {}, {}
 
-        nc.vector.memset(gs_raw[:].rearrange("p g n -> p (g n)").bitcast(I32), 0)
-        make_identity(nc, ident[:])
-
-        def ld(o, i):
-            nc.sync.dma_start(out=o, in_=i)
-
-        def ld_jac(n, g):
-            ld(jac_raw[n][g][:], jac[512 * g : 512 * g + 512, 512 * n : 512 * n + 512].rearrange("(p j) w -> p j w", j=4))
-
-        def ld_scales():
-            rows = g_scales.rearrange("g (Q r) n -> r Q g n", r=4)
-            for r in range(4):
-                ld(gs_raw[r:128:32, :, :].bitcast(I32), rows[r].bitcast(I32))
-
-        def ld_g(h):
-            ld(g_raw[h][:], g_words.rearrange("g p n t -> p g (n t)")[:, :, 2048 * h : 2048 * h + 2048].bitcast(I32))
-
-        def ld_slope(h, c0, c1):
-            ld(slope_sb[h][:, :, c0:c1], slope[512 * h : 512 * h + 512, c0:c1].rearrange("(p t) w -> p t w", t=4))
-
-        def ld_load(n):
-            ld(load_raw[n][:], load[512 * n : 512 * n + 512, :].rearrange("(p j) w -> p j w", j=4))
-
-        def ld_fac(h):
-            ld(fac_raw[h][:], fac[512 * h : 512 * h + 512, :].rearrange("(p j) w -> p j w", j=4))
-
-        ld_jac(0, 0)
-        ld_jac(0, 1)
-        ld_g(0)
-        ld_scales()
-        ld_slope(0, 0, 512)
-        ld_jac(1, 0)
-        ld_jac(1, 1)
-        ld_slope(0, 512, 1024)
-        ld_load(0)
-        ld_load(1)
-        ld(rate_bf[:, 0:16].rearrange("p (h t) -> p h t", t=4), rate_day.rearrange("(h p t) -> p h t", h=4, t=4))
-        ld(rate_bf[:, 16:24].rearrange("p (n c) -> p n c", c=4), rate_node.rearrange("(n m c) -> m n c", n=2, c=4))
-        ld_g(1)
-        ld_slope(1, 0, 1024)
-        ld_fac(0)
-        ld_g(2)
-        ld_slope(2, 0, 1024)
-        ld_fac(1)
-        ld_g(3)
-        ld_slope(3, 0, 1024)
-        ld_fac(2)
-        ld_fac(3)
-
-        def interleave(raw, vcols):
-            grouped = work.tile([128, 512, 4], BF16, name="grouped", align_bytes=64)
-            src = raw[:].rearrange("p j (c i) -> p c j i", i=4)
-            dst = grouped[:].rearrange("p (c i) j -> p c j i", i=4)
-            for eng, c0, c1 in ((vcopy, 0, vcols // 4), (scopy, vcols // 4, (vcols // 4 + 128) // 2), (scopy, (vcols // 4 + 128) // 2, 128)):
-                if c1 > c0:
-                    eng(dst[:, c0:c1], src[:, c0:c1])
-            return grouped
-
-        def quant(grouped, q, fmt):
-            nc.vector.quantize_mx(out=q[0][:].bitcast(fmt), scales=q[1][:], in_=grouped[:].rearrange("p c j -> p (c j)"))
-
-        def perm_g(h):
-            vcopy(g_perm[h][:], g_raw[h][:].rearrange("p g (m t) -> p g t m", t=4))
-            vcopy(gs_perm[h][:], gs_raw[:, :, 512 * h : 512 * h + 512].rearrange("p g (m t) -> p g t m", t=4))
-
-        zn = {}
-        zbg = {}
-        zag = {}
-        s1 = {}
-
-        def stage1(h, n):
-            for t in range(4):
-                acc = psum.tile([128, 512], F32, name="s1", bufs=4)
-                for g in range(2):
-                    nc.tensor.matmul_mx(
-                        out=acc[:],
-                        lhsT=g_perm[h][:, g, t, :].bitcast(E5), lhsT_scale=gs_perm[h][:, g, t, :],
-                        rhs=jac_q[n][g][0][:].bitcast(E4), rhs_scale=jac_q[n][g][1][:],
-                        start=(g == 0), stop=(g == 1),
-                    )
-                s1[h, n, t] = acc
-
-        def mult(h, n):
-            z = work.tile([128, 4, 2, 128, 2], BF16, name="zn", align_bytes=64)
-            for t in range(4):
-                nc.vector.tensor_tensor(
-                    out=z[:, t],
-                    in0=s1[h, n, t][:].rearrange("p (m u e) -> p u m e", u=2, e=2),
-                    in1=slope_sb[h][:, t, 512 * n : 512 * n + 512].rearrange("p (m u e) -> p u m e", u=2, e=2),
-                    op=MULT,
-                )
-            zn[h, n] = z
-
-        def zb_half(h, n, u, eng):
-            if u == 0:
-                zbg[h, n] = work.tile([128, 2, 2, 128, 4], BF16, name="zbg", align_bytes=64)
-            eng(zbg[h, n][:, u], zn[h, n][:, :, u].rearrange("p t m e -> p e m t"))
-
-        def zb_quant(h, n):
-            q = zb_q[h][n]
-            nc.vector.quantize_mx(out=q[0][:].bitcast(E5), scales=q[1][:], in_=zbg[h, n][:].rearrange("p u e m t -> p (u e m t)"))
-
-        def turn(h, n, engs):
-            za = work.tile([128, 512, 4], BF16, name="zag", align_bytes=64)
-            words = za[:].rearrange("p c t -> p (c t)").bitcast(F32).rearrange("p (v t m u) -> p v t m u", v=2, t=2, u=2)
-            z = zn[h, n]
-            for v in range(2):
-                tp = psum.tile([128, 2, 2, 128], F32, name="tp", bufs=2)
-                for t in range(2):
-                    for u in range(2):
-                        nc.tensor.transpose(tp[:, t, u, :], z[:, 2 * v + t, u].rearrange("p m e -> p (m e)").bitcast(F32), ident[:])
-                engs[v](words[:, v], tp[:].rearrange("p t u m -> p t m u"))
-            zag[h, n] = za
-
-        def za_quant(h, n):
-            q = (work.tile([128, 512], U32, name="zaq", bufs=4, align_bytes=64), work.tile([128, 512], U8, name="zas", bufs=4, align_bytes=64))
-            quant(zag[h, n], q, E5)
-            za_q[h, n] = q
-
-        ofac = {}
-
-        def evac(eng, o, acc, col):
-            if eng == "s":
-                nc.scalar.activation(out=o, in_=acc, func=COPY, scale=rate[:, col : col + 1])
+        def copy(engine, out, in_):
+            if engine == "V":
+                nc.vector.tensor_copy(out=out, in_=in_)
+            elif engine == "S":
+                nc.scalar.copy(out=out, in_=in_)
             else:
-                nc.vector.tensor_scalar(out=o, in0=acc, scalar1=rate[:, col : col + 1], scalar2=None, op0=MULT)
+                nc.gpsimd.tensor_scalar(out=out, in0=in_, scalar1=1.0, scalar2=0.0, op0=MULT, op1=ADD)
 
-        def dfac(h, engs, split):
-            o = work.tile([128, 4, 512], F32, name="ofac", align_bytes=64)
-            rows = out_0[512 * h : 512 * h + 512, :].rearrange("(p t) f -> p t f", t=4)
-            for t in range(4):
-                acc = psum.tile([128, 512], F32, name="o", bufs=2)
-                for n in range(2):
-                    q = za_q[h, n]
-                    nc.tensor.matmul_mx(
-                        out=acc[:],
-                        lhsT=q[0][:, 128 * t : 128 * t + 128].bitcast(E5), lhsT_scale=q[1][:, 128 * t : 128 * t + 128],
-                        rhs=load_q[n][0][:].bitcast(E4), rhs_scale=load_q[n][1][:],
-                        start=(n == 0), stop=(n == 1),
-                    )
-                evac(engs[t], o[:, t, :], acc[:], 4 * h + t)
-                if split:
-                    nc.sync.dma_start(out=rows[:, t, :], in_=o[:, t, :])
-            if not split:
-                nc.sync.dma_start(out=rows, in_=o[:])
+        def quantise(values, q, fmt):
+            nc.vector.quantize_mx(out=q[0][:].bitcast(fmt), scales=q[1][:], in_=values)
 
-        def dload_pass(acc, n, c, h):
-            q = zb_q[h][n]
+        def add_product(out, stationary, moving, start, stop):
             nc.tensor.matmul_mx(
-                out=acc[:],
-                lhsT=q[0][:, 128 * c : 128 * c + 128].bitcast(E5), lhsT_scale=q[1][:, 128 * c : 128 * c + 128],
-                rhs=fac_q[h][0][:].bitcast(E4), rhs_scale=fac_q[h][1][:],
-                start=(h == 0), stop=(h == 3),
+                out=out, lhsT=stationary[0].bitcast(E5M2), lhsT_scale=stationary[1],
+                rhs=moving[0][:].bitcast(E4M3), rhs_scale=moving[1][:], start=start, stop=stop,
             )
 
-        def dload_out(acc, n, c, eng):
-            o = work.tile([128, 512], F32, name="oload", bufs=6, align_bytes=64)
-            evac(eng, o[:], acc[:], 16 + 4 * n + c)
-            nc.sync.dma_start(out=out_1[512 * n : 512 * n + 512, :].rearrange("(m c) f -> m c f", c=4)[:, c, :], in_=o[:])
+        def tile_of(q, i):
+            return [part[:, 128 * i : 128 * i + 128] for part in q]
 
-        quant(interleave(jac_raw[0][0], 352), jac_q[0][0], E4)
-        perm_g(0)
-        quant(interleave(jac_raw[0][1], 352), jac_q[0][1], E4)
-        stage1(0, 0)
-        j10 = interleave(jac_raw[1][0], 0)
-        mult(0, 0)
-        j11 = interleave(jac_raw[1][1], 256)
-        quant(j10, jac_q[1][0], E4)
-        quant(j11, jac_q[1][1], E4)
-        zb_half(0, 0, 0, vcopy)
-        zb_half(0, 0, 1, scopy)
+        def empty(engine, out, acc, column):
+            rate = rates[:, column : column + 1]
+            if engine == "V":
+                nc.vector.tensor_scalar(out=out, in0=acc, scalar1=rate, scalar2=None, op0=MULT)
+            else:
+                nc.scalar.activation(out=out, in_=acc, func=COPY, scale=rate)
 
-        vcopy(rate[:], rate_bf[:])
-        steps = [(h, n) for h in range(4) for n in range(2)]
-        for i in range(1, 8):
-            h, n = steps[i]
-            ph, pn = steps[i - 1]
-            stage1(h, n)
-            turn(ph, pn, (scopy, scopy))
-            if n == 1 and h > 0:
-                dfac(h - 1, "ssss", False)
-            if i == 1:
-                l0 = interleave(load_raw[0], 0)
-            if n == 1 and h < 3:
-                perm_g(h + 1)
-            mult(h, n)
-            zb_half(h, n, 0, vcopy)
-            zb_half(h, n, 1, scopy)
-            za_quant(ph, pn)
-            zb_quant(ph, pn)
-            if i == 1:
-                quant(l0, load_q[0], E4)
-                l1 = interleave(load_raw[1], 0)
-                quant(l1, load_q[1], E4)
-            if i in (3, 4, 5, 6):
-                f = interleave(fac_raw[i - 3], 0)
-                quant(f, fac_q[i - 3], E4)
-        turn(3, 1, (scopy, scopy))
-        for c in range(4):
-            acc = psum.tile([128, 512], F32, name="o", bufs=2)
-            for hh in range(4):
-                dload_pass(acc, 0, c, hh)
-            if c == 0:
-                za_quant(3, 1)
-            if c == 1:
-                zb_quant(3, 1)
-            dload_out(acc, 0, c, "sv"[c % 2])
-        accs = []
-        for c in range(4):
-            acc = psum.tile([128, 512], F32, name="s1", bufs=4)
-            for hh in range(3):
-                dload_pass(acc, 1, c, hh)
-            accs.append(acc)
-        dfac(3, "svsv", True)
-        for c in range(4):
-            dload_pass(accs[c], 1, c, 3)
-            dload_out(accs[c], 1, c, "sv"[c % 2])
+        def rows_of_four(matrix):
+            return matrix.rearrange("(p j) w -> p j w", j=4)
+
+        def issue(item):
+            kind, index = item[0], item[1:]
+            block = slice(512 * index[0], 512 * index[0] + 512) if index else None
+            second = slice(512 * index[1], 512 * index[1] + 512) if len(index) == 2 else None
+            if kind == "jac":
+                tile = kept(f"jac{index[0]}", [128, 4, 1024], BF16)
+                nc.sync.dma_start(out=tile[:], in_=rows_of_four(jac[block, :]))
+                for n in range(2):
+                    raw["jac", n, index[0]] = tile[:, :, 512 * n : 512 * n + 512]
+            elif kind in ("load", "fac"):
+                tile = working("raw", [128, 4, 512], BF16, RAW)
+                nc.sync.dma_start(out=tile[:], in_=rows_of_four((load if kind == "load" else fac)[block, :]))
+                raw[item] = tile[:]
+            elif kind == "half slope":
+                tile = kept(f"slope{index[1]}", [128, 4, 512], BF16)
+                nc.sync.dma_start(out=tile[:], in_=rows_of_four(slope[block, second]))
+                slopes[index] = tile[:]
+            elif kind == "slope":
+                tile = working("slope", [128, 4, 1024], BF16, SLOPES)
+                nc.sync.dma_start(out=tile[:], in_=rows_of_four(slope[block, :]))
+                for n in range(2):
+                    slopes[index[0], n] = tile[:, :, 512 * n : 512 * n + 512]
+            elif kind == "g":
+                h, g = index
+                words = g_words[g].rearrange("p d t -> p (d t)")[:, 2048 * h : 2048 * h + 2048]
+                nc.sync.dma_start(out=g_raw[index][:], in_=words.bitcast(I32))
+            elif kind == "scales in":
+                by_row = g_scales.rearrange("g (Q r) d -> r Q g d", r=4)
+                for r in range(4):
+                    nc.sync.dma_start(out=g_scales_raw[r:128:32, :, :].bitcast(I32), in_=by_row[r].bitcast(I32))
+            else:
+                for first, count, vector in ((0, 4, rate_day), (16, 2, rate_node)):
+                    target = rates_in[:, first : first + 4 * count].rearrange("p (b c) -> p b c", c=4)
+                    nc.sync.dma_start(out=target, in_=vector.rearrange("(b p c) -> p b c", b=count, c=4))
+
+        def run(unit, engine):
+            kind, index = unit[0], unit[1:]
+            word = kind.split(" ")
+            if word[0] == "interleave":
+                key, half = (word[1],) + index[:-1], index[-1]
+                if key not in grouped:
+                    grouped[key] = working("grouped", [128, 512, 4], BF16, GROUPED)
+                width = share_of(key, half)[1] // 4
+                part = slice(128 - width, 128) if half else slice(0, width)
+                out = grouped[key][:].rearrange("p (c i) j -> p c j i", i=4)[:, part]
+                copy(engine, out, raw[key].rearrange("p j (c i) -> p c j i", i=4)[:, part])
+            elif kind == "quantise nodes":
+                quantise(by_nodes[index[0]][:].rearrange("p v c t -> p (v c t)"), by_nodes_q[index[0]], E5M2)
+            elif kind == "quantise days":
+                quantise(by_days[index[0]][:].rearrange("p u e m t -> p (u e m t)"), by_days_q[index[0]], E5M2)
+            elif word[0] == "quantise":
+                key = (word[1],) + index
+                quantise(grouped[key][:].rearrange("p c j -> p (c j)"), inputs_q[key], E4M3)
+            elif kind == "codes":
+                copy(engine, g_codes[index][:], g_raw[index][:].rearrange("p (m t) -> p t m", t=4))
+            elif kind == "scales":
+                days = g_scales_raw[:, :, 512 * index[0] : 512 * index[0] + 512]
+                copy(engine, g_scale_rows[index[0]][:], days.rearrange("p g (m t) -> p g t m", t=4))
+            elif kind == "rates":
+                copy(engine, rates[:], rates_in[:])
+            elif kind == "sum":
+                k, t, g = index
+                h, n = STEPS[k]
+                if g == 0:
+                    sums[k, t] = psum.tile([128, 512], F32, name="sums", bufs=SUM_BANKS)
+                stationary = g_codes[h, g][:, t, :], g_scale_rows[h][:, g, t, :]
+                add_product(sums[k, t][:], stationary, inputs_q["jac", n, g], g == 0, g == 1)
+            elif kind == "multiply":
+                k, t = index
+                if k not in products:
+                    products[k] = working("products", [128, 4, 2, 128, 2], BF16, PRODUCTS)
+                in0 = sums[k, t][:].rearrange("p (m u e) -> p u m e", u=2, e=2)
+                in1 = slopes[STEPS[k]][:, t, :].rearrange("p (m u e) -> p u m e", u=2, e=2)
+                nc.vector.tensor_tensor(out=products[k][:, t], in0=in0, in1=in1, op=MULT)
+            elif kind == "turn":
+                k = index[0]
+                for v in range(2):
+                    turned[k, v] = psum.tile([128, 2, 2, 128], F32, name="turns", bufs=TURN_BANKS)
+                    for t in range(2):
+                        for u in range(2):
+                            words = products[k][:, 2 * v + t, u].rearrange("p m e -> p (m e)").bitcast(F32)
+                            nc.tensor.transpose(turned[k, v][:, t, u, :], words, identity[:])
+            elif kind == "turned":
+                k, v = index
+                if k not in by_nodes:
+                    by_nodes[k] = working("by_nodes", [128, 2, 256, 4], BF16, BY_NODES)
+                words = by_nodes[k][:, v].rearrange("p c t -> p (c t)").bitcast(F32)
+                copy(engine, words.rearrange("p (t d u) -> p t d u", t=2, u=2), turned[k, v][:].rearrange("p t u d -> p t d u"))
+            elif kind == "days":
+                k, u = index
+                if k not in by_days:
+                    by_days[k] = working("by_days", [128, 2, 2, 128, 4], BF16, BY_DAYS)
+                copy(engine, by_days[k][:, u], products[k][:, :, u].rearrange("p t m e -> p e m t"))
+            elif kind == "fac sum":
+                h, t = index
+                sums[unit] = psum.tile([128, 512], F32, name="sums", bufs=SUM_BANKS)
+                for n in range(2):
+                    add_product(sums[unit][:], tile_of(by_nodes_q[2 * h + n], t), inputs_q["load", n], n == 0, n == 1)
+            elif kind == "fac out":
+                h, t = index
+                if h not in out_block:
+                    out_block[h] = working("out_block", [128, 4, 512], F32, OUT_BLOCKS)
+                    block_filled[h] = 0
+                rows = rows_of_four(out_0[512 * h : 512 * h + 512, :])
+                empty(engine, out_block[h][:, t, :], sums["fac sum", h, t][:], 4 * h + t)
+                block_filled[h] += 1
+                if h == 3:
+                    nc.sync.dma_start(out=rows[:, t, :], in_=out_block[h][:, t, :])
+                elif block_filled[h] == 4:
+                    nc.sync.dma_start(out=rows, in_=out_block[h][:])
+            elif kind == "load sum":
+                n, c, h = index
+                if h == 0:
+                    sums[kind, n, c] = psum.tile([128, 512], F32, name="sums", bufs=SUM_BANKS)
+                add_product(sums[kind, n, c][:], tile_of(by_days_q[2 * h + n], c), inputs_q["fac", h], h == 0, h == 3)
+            else:
+                n, c = index
+                out = working("out_tile", [128, 512], F32, OUT_TILES)
+                empty(engine, out[:], sums["load sum", n, c][:], 16 + 4 * n + c)
+                nc.sync.dma_start(out=rows_of_four(out_1[512 * n : 512 * n + 512, :])[:, c, :], in_=out[:])
+
+        nc.vector.memset(g_scales_raw[:].rearrange("p g d -> p (g d)").bitcast(I32), 0)
+        make_identity(nc, identity[:])
+
+        units, order, gone = list_units(), plan()[0], set()
+        waiting, issued = list(LOADS), {"raw": [], "slope": []}
+
+        def issue_loads():
+            while waiting:
+                item = waiting[0]
+                tag = {"load": "raw", "fac": "raw", "slope": "slope"}.get(item[0])
+                if tag:
+                    bufs = RAW if tag == "raw" else SLOPES
+                    if len(issued[tag]) >= bufs:
+                        old = issued[tag][len(issued[tag]) - bufs]
+                        if tag == "slope":
+                            last = [("multiply", 2 * old[1] + n, t) for n in range(2) for t in range(4)]
+                        else:
+                            last = [("quantise " + old[0],) + old[1:]]
+                        if not all([unit in gone for unit in last]):
+                            return
+                    issued[tag].append(item)
+                issue(waiting.pop(0))
+
+        issue_loads()
+        for unit in order:
+            run(unit, units[unit][0])
+            gone.add(unit)
+            issue_loads()

@@ -20,43 +20,41 @@ COPY = mybir.ActivationFunctionType.Copy
 STEPS = [(h, n) for h in range(4) for n in range(2)]
 OPERANDS = [("jac", n, g) for n in range(2) for g in range(2)] + [("load", n) for n in range(2)] + [("fac", h) for h in range(4)]
 
-GROUPED, PRODUCTS, BY_DAYS, BY_NODES, RAW, SLOPES = 3, 4, 3, 2, 3, 2
+GROUPED, PRODUCTS, BY_DAYS, BY_NODES, RAW, SLOPES = 3, 4, 3, 2, 7, 6
 SUM_BANKS, TURN_BANKS, OUT_BLOCKS, OUT_TILES = 6, 2, 2, 7
 
 LOADS = [
-    ("jac", 0), ("scales in",), ("jac", 1), ("g", 0, 0), ("g", 0, 1), ("half slope", 0, 1),
-    ("half slope", 0, 0), ("load", 0), ("load", 1), ("g", 1, 1), ("g", 1, 0), ("slope", 1), ("fac", 0),
-    ("rates in",), ("slope", 2), ("fac", 1), ("g", 2, 0), ("g", 2, 1), ("g", 3, 0), ("g", 3, 1), ("slope", 3),
-    ("fac", 2), ("fac", 3),
+    ("jac", 0, 0), ("scales in",), ("jac", 1, 1), ("g", 0, 0), ("g", 0, 1), ("jac", 0, 1), ("jac", 1, 0),
+    ("slope", 0, 0), ("load", 0), ("g", 2, 1), ("slope", 0, 1), ("g", 1, 0), ("g", 1, 1), ("load", 1),
+    ("rates in",), ("slope", 1, 0), ("fac", 0), ("slope", 2, 0), ("slope", 1, 1), ("g", 3, 0), ("fac", 1),
+    ("g", 2, 0), ("g", 3, 1), ("slope", 2, 1), ("slope", 3, 1), ("slope", 3, 0), ("fac", 2), ("fac", 3),
 ]
 
-WINDOW = 0
 ORDER = {
-    "T": ["fac sum", "turn", "load sum", "sum"],
-    "V": ["quantise days", "interleave fac", "codes", "quantise jac", "quantise nodes", "quantise load",
-          "interleave jac", "multiply", "quantise fac", "rates", "scales", "days", "fac out", "load out"],
-    "S": ["fac out", "load out", "turned", "interleave load", "interleave jac", "days", "interleave fac"],
+    "T": ["turn", "fac sum", "sum", "load sum"],
+    "V": ["quantise jac", "fac out", "codes", "scales", "quantise nodes", "load out", "multiply",
+          "quantise load", "interleave jac", "quantise fac", "quantise days", "rates", "interleave fac", "days"],
+    "S": ["fac out", "turned", "interleave load", "days", "interleave jac", "interleave fac", "load out"],
     "G": ["interleave fac"],
 }
 
-JAC_V = [256, 256, 256, 64]
-FAC_V, FAC_G = [(3, 1)], [(2, 0), (2, 1), (3, 0), (1, 0), (0, 1)]
-DAYS_V = [1, 0, 0, 1, 0, 2, 0, 2]
-FAC_OUT_V, LOAD_OUT_V = [(1, 1), (2, 3), (2, 2)], [(1, 3), (1, 2), (1, 0), (1, 1)]
-OPEN_SUMS = 4
+JAC_V = [256, 384, 192, 128]
+FAC_V, FAC_G = [(3, 1)], [(2, 0), (2, 1), (1, 0), (0, 1), (3, 0)]
+DAYS_V = [1, 0, 0, 1, 0, 2, 0, 0]
+FAC_OUT_V, LOAD_OUT_V = [(2, 0), (1, 2), (3, 0), (3, 3)], [(0, 3), (1, 3), (0, 1), (1, 1)]
 
-LENGTH = {"move": 512, "multiply": 512, "quantise": 528, "interleave V": 592, "interleave S": 1072, "interleave G": 1312,
-          "codes": 260, "scales": 504, "rates": 48, "pass": 256, "turn": 584, "switch": 112, "store": 544}
-LOAD_LENGTH = {"jac": 2010, "half slope": 1224, "slope": 2010, "load": 1036, "fac": 1036, "g": 552, "scales in": 280, "rates in": 224}
-LOAD_START, LOAD_END = 660, 1112
-LAG = {"TT": 0, "TV": 336, "TS": 336, "VT": 280, "ST": 280, "VV": 200, "VS": 136, "SV": 68, "SS": 168, "GV": 168, "VG": 168}
+WEIGHT = {"move": 8, "multiply": 8, "quantise": 8, "interleave V": 9, "interleave S": 17, "interleave G": 20,
+          "codes": 4, "scales": 8, "rates": 1, "pass": 4, "turn": 9}
+LOAD_WEIGHT = {"jac": 19, "slope": 19, "load": 16, "fac": 16, "g": 9, "scales in": 4, "rates in": 3}
+LOAD_START, LOAD_END, SWITCH = 10, 17, 2
+MARGIN = {"TT": 0, "TV": 5, "TS": 5, "VT": 4, "ST": 4, "VV": 3, "VS": 2, "SV": 1, "SS": 3, "GV": 3, "VG": 3}
 
 
 def list_units():
     units = {}
 
-    def add(name, engine, length, needs, opens=None, frees=None):
-        units[name] = (engine, length, needs, opens, frees)
+    def add(name, engine, weight, needs, opens=None, frees=None):
+        units[name] = (engine, weight, needs, opens, frees)
 
     for i, key in enumerate(OPERANDS):
         free = [("quantise " + OPERANDS[i - GROUPED][0],) + OPERANDS[i - GROUPED][1:]] if i >= GROUPED else []
@@ -65,41 +63,41 @@ def list_units():
             engine, columns = share_of(key, half)
             if columns:
                 parts.append(("interleave " + key[0],) + key[1:] + (half,))
-                add(parts[-1], engine, LENGTH["interleave " + engine] * columns // 256, [key] + free)
-        add(("quantise " + key[0],) + key[1:], "V", LENGTH["quantise"], parts)
-    add(("rates",), "V", LENGTH["rates"], [("rates in",)])
+                add(parts[-1], engine, WEIGHT["interleave " + engine] * columns / 256, [key] + free)
+        add(("quantise " + key[0],) + key[1:], "V", WEIGHT["quantise"], parts)
+    add(("rates",), "V", WEIGHT["rates"], [("rates in",)])
     for h in range(4):
         for g in range(2):
-            add(("codes", h, g), "V", LENGTH["codes"], [("g", h, g)])
-        add(("scales", h), "V", LENGTH["scales"], [("scales in",)])
+            add(("codes", h, g), "V", WEIGHT["codes"], [("g", h, g)])
+        add(("scales", h), "V", WEIGHT["scales"], [("scales in",)])
     for k, (h, n) in enumerate(STEPS):
-        products = [("multiply", k, t) for t in range(4)]
+        multiplied = [("multiply", k, t) for t in range(4)]
         for t in range(4):
-            add(("sum", k, t, 0), "T", LENGTH["pass"], [("codes", h, 0), ("scales", h), ("quantise jac", n, 0)], opens=("sums", 1))
-            add(("sum", k, t, 1), "T", LENGTH["pass"], [("sum", k, t, 0), ("codes", h, 1), ("quantise jac", n, 1)])
+            add(("sum", k, t, 0), "T", WEIGHT["pass"], [("codes", h, 0), ("scales", h), ("quantise jac", n, 0)], opens=("sums", 1))
+            add(("sum", k, t, 1), "T", WEIGHT["pass"], [("sum", k, t, 0), ("codes", h, 1), ("quantise jac", n, 1)])
             free = [("turn", k - PRODUCTS), ("days", k - PRODUCTS, 0), ("days", k - PRODUCTS, 1)] if k >= PRODUCTS else []
-            add(products[t], "V", LENGTH["multiply"], [("sum", k, t, 1), ("slope", h, n)] + free, frees="sums")
-        add(("turn", k), "T", LENGTH["turn"], products, opens=("turns", 2))
+            add(multiplied[t], "V", WEIGHT["multiply"], [("sum", k, t, 1), ("slope", h, n)] + free, frees="sums")
+        add(("turn", k), "T", WEIGHT["turn"], multiplied, opens=("turns", 2))
         for v in range(2):
             free = [("quantise nodes", k - BY_NODES)] if k >= BY_NODES else []
-            add(("turned", k, v), "S", LENGTH["move"], [("turn", k)] + free, frees="turns")
+            add(("turned", k, v), "S", WEIGHT["move"], [("turn", k)] + free, frees="turns")
         for u in range(2):
             engine = "V" if u < DAYS_V[k] else "S"
             free = [("quantise days", k - BY_DAYS)] if k >= BY_DAYS else []
-            add(("days", k, u), engine, LENGTH["interleave " + engine], products + free)
-        add(("quantise nodes", k), "V", LENGTH["quantise"], [("turned", k, 0), ("turned", k, 1)])
-        add(("quantise days", k), "V", LENGTH["quantise"], [("days", k, 0), ("days", k, 1)])
+            add(("days", k, u), engine, WEIGHT["interleave " + engine], multiplied + free)
+        add(("quantise nodes", k), "V", WEIGHT["quantise"], [("turned", k, 0), ("turned", k, 1)])
+        add(("quantise days", k), "V", WEIGHT["quantise"], [("days", k, 0), ("days", k, 1)])
     for h in range(4):
         for t in range(4):
             needs = [("quantise nodes", 2 * h + n) for n in range(2)] + [("quantise load", n) for n in range(2)]
-            add(("fac sum", h, t), "T", 2 * LENGTH["pass"], needs, opens=("sums", 1))
-            add(("fac out", h, t), "V" if (h, t) in FAC_OUT_V else "S", LENGTH["move"], [("fac sum", h, t), ("rates",)], frees="sums")
+            add(("fac sum", h, t), "T", 2 * WEIGHT["pass"], needs, opens=("sums", 1))
+            add(("fac out", h, t), "V" if (h, t) in FAC_OUT_V else "S", WEIGHT["move"], [("fac sum", h, t), ("rates",)], frees="sums")
     for n in range(2):
         for c in range(4):
             for h in range(4):
                 needs = [("quantise days", 2 * h + n), ("quantise fac", h)] + ([("load sum", n, c, h - 1)] if h else [])
-                add(("load sum", n, c, h), "T", LENGTH["pass"], needs, opens=None if h else ("sums", 1))
-            add(("load out", n, c), "V" if (n, c) in LOAD_OUT_V else "S", LENGTH["move"], [("load sum", n, c, 3), ("rates",)], frees="sums")
+                add(("load sum", n, c, h), "T", WEIGHT["pass"], needs, opens=None if h else ("sums", 1))
+            add(("load out", n, c), "V" if (n, c) in LOAD_OUT_V else "S", WEIGHT["move"], [("load sum", n, c, 3), ("rates",)], frees="sums")
     return units
 
 
@@ -114,16 +112,6 @@ def share_of(key, half):
     return "S", 256
 
 
-def parts_of(item):
-    if item[0] == "jac":
-        return [("jac", n, item[1]) for n in range(2)]
-    if item[0] == "slope":
-        return [("slope", item[1], n) for n in range(2)]
-    if item[0] == "half slope":
-        return [("slope",) + item[1:]]
-    return [item]
-
-
 def shares_port(name):
     return name[0] not in ("multiply", "fac out", "load out")
 
@@ -132,21 +120,20 @@ def plan():
     units = list_units()
     arrive, clock = {}, LOAD_START
     for item in LOADS:
-        clock += LOAD_LENGTH[item[0]]
-        for part in parts_of(item):
-            arrive[part] = clock + LOAD_END
+        clock += LOAD_WEIGHT[item[0]]
+        arrive[item] = clock + LOAD_END
 
     users, missing, ready = {}, {}, {}
     done, order = {}, []
     free_at = {"T": 0, "V": 0, "S": 0, "G": 0}
     banks = {"sums": [0] * SUM_BANKS, "turns": [0] * TURN_BANKS}
-    port_free, stored, turning, open_sums = 0, clock, False, 0
+    port_free, turning = 0, False
 
-    def lag(need, engine):
-        return arrive[need] if need in arrive else done[need] + LAG[units[need][0] + engine]
+    def usable(need, engine):
+        return arrive[need] if need in arrive else done[need] + MARGIN[units[need][0] + engine]
 
     def make_ready(name):
-        ready[name] = max([lag(need, units[name][0]) for need in units[name][2]])
+        ready[name] = max([usable(need, units[name][0]) for need in units[name][2]])
 
     for name in units:
         inside = [need for need in units[name][2] if need not in arrive]
@@ -159,25 +146,22 @@ def plan():
     while ready:
         choices = []
         for name in ready:
-            engine, length, needs, opens, frees = units[name]
+            engine, weight, needs, opens, frees = units[name]
             start = max(free_at[engine], ready[name])
             if opens:
                 if len(banks[opens[0]]) < opens[1]:
-                    continue
-                if name[0] == "load sum" and open_sums >= OPEN_SUMS and ("multiply", 7, 3) not in done:
                     continue
                 start = max(start, sorted(banks[opens[0]])[opens[1] - 1])
             if engine == "G":
                 start = max(start, port_free)
             if engine == "V" and shares_port(name):
                 start = max(start, free_at["G"])
-            choices.append((ORDER[engine].index(name[0]), name[1:], start, name))
-        soonest = min([choice[2] for choice in choices])
-        start, name = min([choice for choice in choices if choice[2] <= soonest + WINDOW])[2:]
-        engine, length, needs, opens, frees = units[name]
-        end = start + length
+            choices.append((start, ORDER[engine].index(name[0]), name[1:], name))
+        start, order_of_kind, indices, name = min(choices)
+        engine, weight, needs, opens, frees = units[name]
+        end = start + weight
         if engine == "T" and (name[0] == "turn") != turning:
-            end += LENGTH["switch"]
+            end += SWITCH
             turning = not turning
         if engine == "V" and shares_port(name):
             port_free = end
@@ -185,17 +169,14 @@ def plan():
         if opens:
             banks[opens[0]] = sorted(banks[opens[0]])[opens[1] :]
         if frees:
-            banks[frees].append(end + LAG["TV"] // 5)
-        open_sums += (name[0] == "load sum" and name[3] == 0) - (name[0] == "load out")
-        if name[0] in ("fac out", "load out"):
-            stored = max(stored, end + LOAD_START) + LENGTH["store"]
+            banks[frees].append(end + 1)
         ready.pop(name)
         order.append((start, len(order), name))
         for user in users.get(name, []):
             missing[user] -= 1
             if missing[user] == 0:
                 make_ready(user)
-    return [name for start, i, name in sorted(order)], stored
+    return [name for start, i, name in sorted(order)]
 
 
 def tile_volatility_calibration_gradients_e3_kernel(
@@ -263,24 +244,13 @@ def tile_volatility_calibration_gradients_e3_kernel(
             kind, index = item[0], item[1:]
             block = slice(512 * index[0], 512 * index[0] + 512) if index else None
             second = slice(512 * index[1], 512 * index[1] + 512) if len(index) == 2 else None
-            if kind == "jac":
-                tile = kept(f"jac{index[0]}", [128, 4, 1024], BF16)
-                nc.sync.dma_start(out=tile[:], in_=rows_of_four(jac[block, :]))
-                for n in range(2):
-                    raw["jac", n, index[0]] = tile[:, :, 512 * n : 512 * n + 512]
-            elif kind in ("load", "fac"):
-                tile = working("raw", [128, 4, 512], BF16, RAW)
-                nc.sync.dma_start(out=tile[:], in_=rows_of_four((load if kind == "load" else fac)[block, :]))
-                raw[item] = tile[:]
-            elif kind == "half slope":
-                tile = kept(f"slope{index[1]}", [128, 4, 512], BF16)
-                nc.sync.dma_start(out=tile[:], in_=rows_of_four(slope[block, second]))
-                slopes[index] = tile[:]
+            if kind in ("jac", "load", "fac"):
+                raw[item] = working("raw", [128, 4, 512], BF16, RAW)
+                source = jac[second, block] if kind == "jac" else load[block, :] if kind == "load" else fac[block, :]
+                nc.sync.dma_start(out=raw[item][:], in_=rows_of_four(source))
             elif kind == "slope":
-                tile = working("slope", [128, 4, 1024], BF16, SLOPES)
-                nc.sync.dma_start(out=tile[:], in_=rows_of_four(slope[block, :]))
-                for n in range(2):
-                    slopes[index[0], n] = tile[:, :, 512 * n : 512 * n + 512]
+                slopes[index] = working("slope", [128, 4, 512], BF16, SLOPES)
+                nc.sync.dma_start(out=slopes[index][:], in_=rows_of_four(slope[block, second]))
             elif kind == "g":
                 h, g = index
                 words = g_words[g].rearrange("p d t -> p (d t)")[:, 2048 * h : 2048 * h + 2048]
@@ -304,7 +274,7 @@ def tile_volatility_calibration_gradients_e3_kernel(
                 width = share_of(key, half)[1] // 4
                 part = slice(128 - width, 128) if half else slice(0, width)
                 out = grouped[key][:].rearrange("p (c i) j -> p c j i", i=4)[:, part]
-                copy(engine, out, raw[key].rearrange("p j (c i) -> p c j i", i=4)[:, part])
+                copy(engine, out, raw[key][:].rearrange("p j (c i) -> p c j i", i=4)[:, part])
             elif kind == "quantise nodes":
                 quantise(by_nodes[index[0]][:].rearrange("p v c t -> p (v c t)"), by_nodes_q[index[0]], E5M2)
             elif kind == "quantise days":
@@ -315,8 +285,8 @@ def tile_volatility_calibration_gradients_e3_kernel(
             elif kind == "codes":
                 copy(engine, g_codes[index][:], g_raw[index][:].rearrange("p (m t) -> p t m", t=4))
             elif kind == "scales":
-                days = g_scales_raw[:, :, 512 * index[0] : 512 * index[0] + 512]
-                copy(engine, g_scale_rows[index[0]][:], days.rearrange("p g (m t) -> p g t m", t=4))
+                of_block = g_scales_raw[:, :, 512 * index[0] : 512 * index[0] + 512]
+                copy(engine, g_scale_rows[index[0]][:], of_block.rearrange("p g (m t) -> p g t m", t=4))
             elif kind == "rates":
                 copy(engine, rates[:], rates_in[:])
             elif kind == "sum":
@@ -383,19 +353,19 @@ def tile_volatility_calibration_gradients_e3_kernel(
         nc.vector.memset(g_scales_raw[:].rearrange("p g d -> p (g d)").bitcast(I32), 0)
         make_identity(nc, identity[:])
 
-        units, order, gone = list_units(), plan()[0], set()
+        units, order, gone = list_units(), plan(), set()
         waiting, issued = list(LOADS), {"raw": [], "slope": []}
 
         def issue_loads():
             while waiting:
                 item = waiting[0]
-                tag = {"load": "raw", "fac": "raw", "slope": "slope"}.get(item[0])
+                tag = {"jac": "raw", "load": "raw", "fac": "raw", "slope": "slope"}.get(item[0])
                 if tag:
                     bufs = RAW if tag == "raw" else SLOPES
                     if len(issued[tag]) >= bufs:
                         old = issued[tag][len(issued[tag]) - bufs]
                         if tag == "slope":
-                            last = [("multiply", 2 * old[1] + n, t) for n in range(2) for t in range(4)]
+                            last = [("multiply", STEPS.index(old[1:]), t) for t in range(4)]
                         else:
                             last = [("quantise " + old[0],) + old[1:]]
                         if not all([unit in gone for unit in last]):

from contextlib import ExitStack

import concourse.mybir as mybir
from concourse.masks import make_identity

D, Q, P, F = 2048, 1024, 1024, 512
FLOPS = 2 * D * Q * P + 2 * 2 * D * P * F

F32 = mybir.dt.float32
BF16 = mybir.dt.bfloat16
I32 = mybir.dt.int32
U32 = mybir.dt.uint32
U8 = mybir.dt.uint8
E4M3 = mybir.dt.float8_e4m3fn_x4
E5M2 = mybir.dt.float8_e5m2_x4
MULT = mybir.AluOpType.mult
ADD = mybir.AluOpType.add
COPY = mybir.ActivationFunctionType.Copy

STEPS = [(h, n) for h in range(4) for n in range(2)]
OPERANDS = [("jac", n, g) for n in range(2) for g in range(2)] + [("load", n) for n in range(2)] + [("fac", h) for h in range(4)]

GROUPED, PRODUCTS, BY_DAYS, BY_NODES, RAW, SLOPES = 3, 4, 3, 2, 7, 6
SUM_BANKS, TURN_BANKS, OUT_BLOCKS, OUT_TILES = 6, 2, 2, 7

LOADS = [
    ("jac", 0, 0), ("scales in",), ("jac", 1, 1), ("g", 0, 0), ("g", 0, 1), ("jac", 0, 1), ("jac", 1, 0),
    ("slope", 0, 0), ("load", 0), ("g", 2, 1), ("slope", 0, 1), ("g", 1, 0), ("g", 1, 1), ("load", 1),
    ("rates in",), ("slope", 1, 0), ("fac", 0), ("slope", 2, 0), ("slope", 1, 1), ("g", 3, 0), ("fac", 1),
    ("g", 2, 0), ("g", 3, 1), ("slope", 2, 1), ("slope", 3, 1), ("slope", 3, 0), ("fac", 2), ("fac", 3),
]

ORDER = {
    "T": ["turn", "fac sum", "sum", "load sum"],
    "V": ["quantise jac", "fac out", "codes", "scales", "quantise nodes", "load out", "multiply",
          "quantise load", "interleave jac", "quantise fac", "quantise days", "rates", "interleave fac", "days"],
    "S": ["fac out", "turned", "interleave load", "days", "interleave jac", "interleave fac", "load out"],
    "G": ["interleave fac"],
}

JAC_V = [256, 384, 192, 128]
FAC_V, FAC_G = [(3, 1)], [(2, 0), (2, 1), (1, 0), (0, 1), (3, 0)]
DAYS_V = [1, 0, 0, 1, 0, 2, 0, 0]
FAC_OUT_V, LOAD_OUT_V = [(2, 0), (1, 2), (3, 0), (3, 3)], [(0, 3), (1, 3), (0, 1), (1, 1)]

WEIGHT = {"move": 8, "multiply": 8, "quantise": 8, "interleave V": 9, "interleave S": 17, "interleave G": 20,
          "codes": 4, "scales": 8, "rates": 1, "pass": 4, "turn": 9}
LOAD_WEIGHT = {"jac": 19, "slope": 19, "load": 16, "fac": 16, "g": 9, "scales in": 4, "rates in": 3}
LOAD_START, LOAD_END, SWITCH = 10, 17, 2
MARGIN = {"TT": 0, "TV": 5, "TS": 5, "VT": 4, "ST": 4, "VV": 3, "VS": 2, "SV": 1, "SS": 3, "GV": 3, "VG": 3}


def list_units():
    units = {}

    def add(name, engine, weight, needs, opens=None, frees=None):
        units[name] = (engine, weight, needs, opens, frees)

    for i, key in enumerate(OPERANDS):
        free = [("quantise " + OPERANDS[i - GROUPED][0],) + OPERANDS[i - GROUPED][1:]] if i >= GROUPED else []
        parts = []
        for half in range(2):
            engine, columns = share_of(key, half)
            if columns:
                parts.append(("interleave " + key[0],) + key[1:] + (half,))
                add(parts[-1], engine, WEIGHT["interleave " + engine] * columns / 256, [key] + free)
        add(("quantise " + key[0],) + key[1:], "V", WEIGHT["quantise"], parts)
    add(("rates",), "V", WEIGHT["rates"], [("rates in",)])
    for h in range(4):
        for g in range(2):
            add(("codes", h, g), "V", WEIGHT["codes"], [("g", h, g)])
        add(("scales", h), "V", WEIGHT["scales"], [("scales in",)])
    for k, (h, n) in enumerate(STEPS):
        multiplied = [("multiply", k, t) for t in range(4)]
        for t in range(4):
            add(("sum", k, t, 0), "T", WEIGHT["pass"], [("codes", h, 0), ("scales", h), ("quantise jac", n, 0)], opens=("sums", 1))
            add(("sum", k, t, 1), "T", WEIGHT["pass"], [("sum", k, t, 0), ("codes", h, 1), ("quantise jac", n, 1)])
            free = [("turn", k - PRODUCTS), ("days", k - PRODUCTS, 0), ("days", k - PRODUCTS, 1)] if k >= PRODUCTS else []
            add(multiplied[t], "V", WEIGHT["multiply"], [("sum", k, t, 1), ("slope", h, n)] + free, frees="sums")
        add(("turn", k), "T", WEIGHT["turn"], multiplied, opens=("turns", 2))
        for v in range(2):
            free = [("quantise nodes", k - BY_NODES)] if k >= BY_NODES else []
            add(("turned", k, v), "S", WEIGHT["move"], [("turn", k)] + free, frees="turns")
        for u in range(2):
            engine = "V" if u < DAYS_V[k] else "S"
            free = [("quantise days", k - BY_DAYS)] if k >= BY_DAYS else []
            add(("days", k, u), engine, WEIGHT["interleave " + engine], multiplied + free)
        add(("quantise nodes", k), "V", WEIGHT["quantise"], [("turned", k, 0), ("turned", k, 1)])
        add(("quantise days", k), "V", WEIGHT["quantise"], [("days", k, 0), ("days", k, 1)])
    for h in range(4):
        for t in range(4):
            needs = [("quantise nodes", 2 * h + n) for n in range(2)] + [("quantise load", n) for n in range(2)]
            add(("fac sum", h, t), "T", 2 * WEIGHT["pass"], needs, opens=("sums", 1))
            add(("fac out", h, t), "V" if (h, t) in FAC_OUT_V else "S", WEIGHT["move"], [("fac sum", h, t), ("rates",)], frees="sums")
    for n in range(2):
        for c in range(4):
            for h in range(4):
                needs = [("quantise days", 2 * h + n), ("quantise fac", h)] + ([("load sum", n, c, h - 1)] if h else [])
                add(("load sum", n, c, h), "T", WEIGHT["pass"], needs, opens=None if h else ("sums", 1))
            add(("load out", n, c), "V" if (n, c) in LOAD_OUT_V else "S", WEIGHT["move"], [("load sum", n, c, 3), ("rates",)], frees="sums")
    return units


def share_of(key, half):
    if key[0] == "jac":
        columns = JAC_V[2 * key[1] + key[2]]
        return ("S", 512 - columns) if half else ("V", columns)
    if key[0] == "fac" and (key[1], half) in FAC_V:
        return "V", 256
    if key[0] == "fac" and (key[1], half) in FAC_G:
        return "G", 256
    return "S", 256


def shares_port(name):
    return name[0] not in ("multiply", "fac out", "load out")


def plan():
    units = list_units()
    arrive, clock = {}, LOAD_START
    for item in LOADS:
        clock += LOAD_WEIGHT[item[0]]
        arrive[item] = clock + LOAD_END

    users, missing, ready = {}, {}, {}
    done, order = {}, []
    free_at = {"T": 0, "V": 0, "S": 0, "G": 0}
    banks = {"sums": [0] * SUM_BANKS, "turns": [0] * TURN_BANKS}
    port_free, turning = 0, False

    def usable(need, engine):
        return arrive[need] if need in arrive else done[need] + MARGIN[units[need][0] + engine]

    def make_ready(name):
        ready[name] = max([usable(need, units[name][0]) for need in units[name][2]])

    for name in units:
        inside = [need for need in units[name][2] if need not in arrive]
        missing[name] = len(inside)
        for need in inside:
            users.setdefault(need, []).append(name)
        if not inside:
            make_ready(name)

    while ready:
        choices = []
        for name in ready:
            engine, weight, needs, opens, frees = units[name]
            start = max(free_at[engine], ready[name])
            if opens:
                if len(banks[opens[0]]) < opens[1]:
                    continue
                start = max(start, sorted(banks[opens[0]])[opens[1] - 1])
            if engine == "G":
                start = max(start, port_free)
            if engine == "V" and shares_port(name):
                start = max(start, free_at["G"])
            choices.append((start, ORDER[engine].index(name[0]), name[1:], name))
        start, order_of_kind, indices, name = min(choices)
        engine, weight, needs, opens, frees = units[name]
        end = start + weight
        if engine == "T" and (name[0] == "turn") != turning:
            end += SWITCH
            turning = not turning
        if engine == "V" and shares_port(name):
            port_free = end
        free_at[engine] = done[name] = end
        if opens:
            banks[opens[0]] = sorted(banks[opens[0]])[opens[1] :]
        if frees:
            banks[frees].append(end + 1)
        ready.pop(name)
        order.append((start, len(order), name))
        for user in users.get(name, []):
            missing[user] -= 1
            if missing[user] == 0:
                make_ready(user)
    return [name for start, i, name in sorted(order)]


def tile_volatility_calibration_gradients_e3_kernel(
    tc, g_words, g_scales, jac, slope, load, fac, rate_day, rate_node, out_0, out_1
):
    nc = tc.nc
    with ExitStack() as ctx:
        keep = ctx.enter_context(tc.tile_pool(name="keep", bufs=1))
        work = ctx.enter_context(tc.tile_pool(name="work", bufs=2))
        psum = ctx.enter_context(tc.psum_pool(name="psum", bufs=2))
        ctx.enter_context(tc.manual_schedule())

        def kept(name, shape, dtype):
            return keep.tile(shape, dtype, name=name, align_bytes=64)

        def working(name, shape, dtype, bufs):
            return work.tile(shape, dtype, name=name, bufs=bufs, align_bytes=64)

        def quantised(name):
            return kept(name + "_codes", [128, 512], U32), kept(name + "_scales", [128, 512], U8)

        identity = kept("identity", [128, 128], F32)
        g_raw = {(h, g): kept(f"g_raw{h}{g}", [128, 512], I32) for h in range(4) for g in range(2)}
        g_codes = {(h, g): kept(f"g_codes{h}{g}", [128, 4, 128], I32) for h in range(4) for g in range(2)}
        g_scales_raw = kept("g_scales_raw", [128, 2, 2048], U8)
        g_scale_rows = [kept(f"g_scale_rows{h}", [128, 2, 4, 128], U8) for h in range(4)]
        inputs_q = {key: quantised("_".join([str(part) for part in key])) for key in OPERANDS}
        by_days_q = [quantised(f"by_days{k}") for k in range(8)]
        by_nodes_q = [quantised(f"by_nodes{k}") for k in range(8)]
        rates_in = kept("rates_in", [128, 24], BF16)
        rates = kept("rates", [128, 24], F32)
        slopes, raw, grouped, sums, products, turned, by_nodes, by_days, out_block, block_filled = {}, {}, {}, {}, {}, {}, {}, {}, {}, {}

        def copy(engine, out, in_):
            if engine == "V":
                nc.vector.tensor_copy(out=out, in_=in_)
            elif engine == "S":
                nc.scalar.copy(out=out, in_=in_)
            else:
                nc.gpsimd.tensor_scalar(out=out, in0=in_, scalar1=1.0, scalar2=0.0, op0=MULT, op1=ADD)

        def quantise(values, q, fmt):
            nc.vector.quantize_mx(out=q[0][:].bitcast(fmt), scales=q[1][:], in_=values)

        def add_product(out, stationary, moving, start, stop):
            nc.tensor.matmul_mx(
                out=out, lhsT=stationary[0].bitcast(E5M2), lhsT_scale=stationary[1],
                rhs=moving[0][:].bitcast(E4M3), rhs_scale=moving[1][:], start=start, stop=stop,
            )

        def tile_of(q, i):
            return [part[:, 128 * i : 128 * i + 128] for part in q]

        def empty(engine, out, acc, column):
            rate = rates[:, column : column + 1]
            if engine == "V":
                nc.vector.tensor_scalar(out=out, in0=acc, scalar1=rate, scalar2=None, op0=MULT)
            else:
                nc.scalar.activation(out=out, in_=acc, func=COPY, scale=rate)

        def rows_of_four(matrix):
            return matrix.rearrange("(p j) w -> p j w", j=4)

        def issue(item):
            kind, index = item[0], item[1:]
            block = slice(512 * index[0], 512 * index[0] + 512) if index else None
            second = slice(512 * index[1], 512 * index[1] + 512) if len(index) == 2 else None
            if kind in ("jac", "load", "fac"):
                raw[item] = working("raw", [128, 4, 512], BF16, RAW)
                source = jac[second, block] if kind == "jac" else load[block, :] if kind == "load" else fac[block, :]
                nc.sync.dma_start(out=raw[item][:], in_=rows_of_four(source))
            elif kind == "slope":
                slopes[index] = working("slope", [128, 4, 512], BF16, SLOPES)
                nc.sync.dma_start(out=slopes[index][:], in_=rows_of_four(slope[block, second]))
            elif kind == "g":
                h, g = index
                words = g_words[g].rearrange("p d t -> p (d t)")[:, 2048 * h : 2048 * h + 2048]
                nc.sync.dma_start(out=g_raw[index][:], in_=words.bitcast(I32))
            elif kind == "scales in":
                by_row = g_scales.rearrange("g (Q r) d -> r Q g d", r=4)
                for r in range(4):
                    nc.sync.dma_start(out=g_scales_raw[r:128:32, :, :].bitcast(I32), in_=by_row[r].bitcast(I32))
            else:
                for first, count, vector in ((0, 4, rate_day), (16, 2, rate_node)):
                    target = rates_in[:, first : first + 4 * count].rearrange("p (b c) -> p b c", c=4)
                    nc.sync.dma_start(out=target, in_=vector.rearrange("(b p c) -> p b c", b=count, c=4))

        def run(unit, engine):
            kind, index = unit[0], unit[1:]
            word = kind.split(" ")
            if word[0] == "interleave":
                key, half = (word[1],) + index[:-1], index[-1]
                if key not in grouped:
                    grouped[key] = working("grouped", [128, 512, 4], BF16, GROUPED)
                width = share_of(key, half)[1] // 4
                part = slice(128 - width, 128) if half else slice(0, width)
                out = grouped[key][:].rearrange("p (c i) j -> p c j i", i=4)[:, part]
                copy(engine, out, raw[key][:].rearrange("p j (c i) -> p c j i", i=4)[:, part])
            elif kind == "quantise nodes":
                quantise(by_nodes[index[0]][:].rearrange("p v c t -> p (v c t)"), by_nodes_q[index[0]], E5M2)
            elif kind == "quantise days":
                quantise(by_days[index[0]][:].rearrange("p u e m t -> p (u e m t)"), by_days_q[index[0]], E5M2)
            elif word[0] == "quantise":
                key = (word[1],) + index
                quantise(grouped[key][:].rearrange("p c j -> p (c j)"), inputs_q[key], E4M3)
            elif kind == "codes":
                copy(engine, g_codes[index][:], g_raw[index][:].rearrange("p (m t) -> p t m", t=4))
            elif kind == "scales":
                of_block = g_scales_raw[:, :, 512 * index[0] : 512 * index[0] + 512]
                copy(engine, g_scale_rows[index[0]][:], of_block.rearrange("p g (m t) -> p g t m", t=4))
            elif kind == "rates":
                copy(engine, rates[:], rates_in[:])
            elif kind == "sum":
                k, t, g = index
                h, n = STEPS[k]
                if g == 0:
                    sums[k, t] = psum.tile([128, 512], F32, name="sums", bufs=SUM_BANKS)
                stationary = g_codes[h, g][:, t, :], g_scale_rows[h][:, g, t, :]
                add_product(sums[k, t][:], stationary, inputs_q["jac", n, g], g == 0, g == 1)
            elif kind == "multiply":
                k, t = index
                if k not in products:
                    products[k] = working("products", [128, 4, 2, 128, 2], BF16, PRODUCTS)
                in0 = sums[k, t][:].rearrange("p (m u e) -> p u m e", u=2, e=2)
                in1 = slopes[STEPS[k]][:, t, :].rearrange("p (m u e) -> p u m e", u=2, e=2)
                nc.vector.tensor_tensor(out=products[k][:, t], in0=in0, in1=in1, op=MULT)
            elif kind == "turn":
                k = index[0]
                for v in range(2):
                    turned[k, v] = psum.tile([128, 2, 2, 128], F32, name="turns", bufs=TURN_BANKS)
                    for t in range(2):
                        for u in range(2):
                            words = products[k][:, 2 * v + t, u].rearrange("p m e -> p (m e)").bitcast(F32)
                            nc.tensor.transpose(turned[k, v][:, t, u, :], words, identity[:])
            elif kind == "turned":
                k, v = index
                if k not in by_nodes:
                    by_nodes[k] = working("by_nodes", [128, 2, 256, 4], BF16, BY_NODES)
                words = by_nodes[k][:, v].rearrange("p c t -> p (c t)").bitcast(F32)
                copy(engine, words.rearrange("p (t d u) -> p t d u", t=2, u=2), turned[k, v][:].rearrange("p t u d -> p t d u"))
            elif kind == "days":
                k, u = index
                if k not in by_days:
                    by_days[k] = working("by_days", [128, 2, 2, 128, 4], BF16, BY_DAYS)
                copy(engine, by_days[k][:, u], products[k][:, :, u].rearrange("p t m e -> p e m t"))
            elif kind == "fac sum":
                h, t = index
                sums[unit] = psum.tile([128, 512], F32, name="sums", bufs=SUM_BANKS)
                for n in range(2):
                    add_product(sums[unit][:], tile_of(by_nodes_q[2 * h + n], t), inputs_q["load", n], n == 0, n == 1)
            elif kind == "fac out":
                h, t = index
                if h not in out_block:
                    out_block[h] = working("out_block", [128, 4, 512], F32, OUT_BLOCKS)
                    block_filled[h] = 0
                rows = rows_of_four(out_0[512 * h : 512 * h + 512, :])
                empty(engine, out_block[h][:, t, :], sums["fac sum", h, t][:], 4 * h + t)
                block_filled[h] += 1
                if h == 3:
                    nc.sync.dma_start(out=rows[:, t, :], in_=out_block[h][:, t, :])
                elif block_filled[h] == 4:
                    nc.sync.dma_start(out=rows, in_=out_block[h][:])
            elif kind == "load sum":
                n, c, h = index
                if h == 0:
                    sums[kind, n, c] = psum.tile([128, 512], F32, name="sums", bufs=SUM_BANKS)
                add_product(sums[kind, n, c][:], tile_of(by_days_q[2 * h + n], c), inputs_q["fac", h], h == 0, h == 3)
            else:
                n, c = index
                out = working("out_tile", [128, 512], F32, OUT_TILES)
                empty(engine, out[:], sums["load sum", n, c][:], 16 + 4 * n + c)
                nc.sync.dma_start(out=rows_of_four(out_1[512 * n : 512 * n + 512, :])[:, c, :], in_=out[:])

        nc.vector.memset(g_scales_raw[:].rearrange("p g d -> p (g d)").bitcast(I32), 0)
        make_identity(nc, identity[:])

        units, order, gone = list_units(), plan(), set()
        waiting, issued = list(LOADS), {"raw": [], "slope": []}

        def issue_loads():
            while waiting:
                item = waiting[0]
                tag = {"jac": "raw", "load": "raw", "fac": "raw", "slope": "slope"}.get(item[0])
                if tag:
                    bufs = RAW if tag == "raw" else SLOPES
                    if len(issued[tag]) >= bufs:
                        old = issued[tag][len(issued[tag]) - bufs]
                        if tag == "slope":
                            last = [("multiply", STEPS.index(old[1:]), t) for t in range(4)]
                        else:
                            last = [("quantise " + old[0],) + old[1:]]
                        if not all([unit in gone for unit in last]):
                            return
                    issued[tag].append(item)
                issue(waiting.pop(0))

        issue_loads()
        for unit in order:
            run(unit, units[unit][0])
            gone.add(unit)
            issue_loads()
